import numpy as np, ml_dtypes
CORES = [13,21,141,149]
N = 4
NH, QP = 4, 32
def setup_inputs(rng):
    q = rng.standard_normal((N, 128, NH * QP), dtype=np.float32) / 4; k = rng.standard_normal((N, 128, NH * 128), dtype=np.float32)
    a = 2 * np.pi * rng.random((N, NH * QP)); s = 400 * rng.random((N, NH * QP)) ** 1.5; q[:, 0, :] = s * np.cos(a); q[:, 1, :] = s * np.sin(a); q[:, 2, :] = 150 * rng.standard_normal((N, NH * QP)); k[:, 2, :] = 1 + k[:, 2, :] / 50
    a = (2 * np.pi * rng.random((1, NH, 1)) + np.pi / 2 * (rng.permuted(np.tile(np.arange(N), (NH, 1)), axis=1).T.reshape(N, NH, 1) + 0.5) / N - 0.5 + rng.random((N, NH, 128))).reshape(N, NH * 128); k[:, 0, :] = np.cos(a); k[:, 1, :] = np.sin(a)
    return {"q": q.astype(ml_dtypes.bfloat16), "k": k.astype(ml_dtypes.bfloat16), "v": rng.standard_normal((N, 128, NH * 128), dtype=np.float32).astype(ml_dtypes.bfloat16)}
def setup_inputs_big(rng):
    d = setup_inputs(rng)
    for k in ("v",): d[k] = (d[k].astype(np.float32) * 1048576.0).astype(d[k].dtype)
    return d
def setup_inputs_small(rng):
    d = setup_inputs(rng)
    for k in ("v",): d[k] = (d[k].astype(np.float32) * (1 / 1048576.0)).astype(d[k].dtype)
    return d
def reference(q, k, v):
    Q, K, V = q.astype(np.float64), k.astype(np.float64), v.astype(np.float64)
    y = np.zeros((N, QP, NH * 128))
    for r in range(N):
        for h in range(NH):
            S = np.concatenate([K[j][:, 128 * h:128 * h + 128].T @ Q[r][:, QP * h:QP * h + QP] for j in range(N)], axis=0)
            P = np.exp(S - S.max(axis=0)); P = P / P.sum(axis=0)
            y[r][:, 128 * h:128 * h + 128] = P.T @ np.concatenate([V[j][:, 128 * h:128 * h + 128] for j in range(N)], axis=0)
    return {"y": y.astype(ml_dtypes.bfloat16)}

@@ -1,0 +1,195 @@
+from concourse.bass import DstId, RemoteDMATransfer
+from concourse.mybir import AluOpType, AxisListType, ActivationFunctionType
+
+NH, QP, KP, FD = 4, 32, 128, 128
+COL_L, COL_M = FD, FD + 1
+WID = FD + 2
+PAD = 136
+
+SCRATCH = {
+    "qs": ("sbuf", [128, NH * QP], "bfloat16"),
+    "qx": ("sbuf", [128, NH * QP], "bfloat16"),
+    "ks": ("sbuf", [128, NH * KP], "bfloat16"),
+    "vs": ("sbuf", [128, NH * FD], "bfloat16"),
+    "msk": ("sbuf", [128, 128], "float32"),
+    "idn": ("sbuf", [128, 128], "bfloat16"),
+    "one": ("sbuf", [128, 128], "bfloat16"),
+    "prm": ("sbuf", [128, 128], "bfloat16"),
+    "p0": ("sbuf", [128, KP], "bfloat16"), "p1": ("sbuf", [128, KP], "bfloat16"),
+    "pt0": ("sbuf", [128, 128], "bfloat16"), "pt1": ("sbuf", [128, 128], "bfloat16"),
+    "lf0": ("sbuf", [128, 4], "float32"), "lf1": ("sbuf", [128, 4], "float32"),
+    "land": ("sbuf", [128, 4, PAD], "bfloat16"),
+    "snd": ("sbuf", [128, PAD], "bfloat16"),
+    "ngm": ("sbuf", [128, 4], "float32"),
+    "aw": ("sbuf", [128, 8], "bfloat16"),
+    "dg": ("sbuf", [128, 4, 128], "bfloat16"),
+    "rl": ("sbuf", [128, 4], "float32"),
+    "ysb": ("sbuf", [128, FD], "bfloat16"),
+    "s0": ("psum", [128, 512], "float32"), "s1": ("psum", [128, 512], "float32"),
+    "o0": ("psum", [128, 512], "float32"), "o1": ("psum", [128, 512], "float32"),
+    "t0": ("psum", [128, 1024], "bfloat16"), "t1": ("psum", [128, 1024], "bfloat16"),
+    "yp": ("psum", [128, 512], "float32"),
+}
+SEMAPHORES = (["lq", "lk", "lv", "aq", "ak", "av", "ax", "ar", "ls", "z", "mk", "id", "on", "pm",
+               "n", "a", "d0", "d1", "d2", "d3", "y", "r", "f", "st"]
+              + [s + i for i in "01" for s in ("ss", "sm", "sp", "st", "sc", "sv", "so")])
+
+
+def plan(T, topo):
+    cores = list(T.cores)
+    world = range((max(topo.host(c) for c in cores) + 1) * topo.CORES_PER_HOST)
+    near, far, hp = {}, {}, {}
+    for r in cores:
+        near[r] = [x for x in cores if x != r and topo.may_write(r, x)]
+        far[r] = [x for x in cores if x != r and not topo.may_write(r, x)]
+        own = [d for d in world if d not in cores and topo.host(d) == topo.host(r) and topo.chip(d) == topo.chip(r)
+               and topo.die(d) == topo.die(r) and all(topo.may_write(d, x) for x in far[r])]
+        for i, x in enumerate(far[r]):
+            hp[(r, x)] = own[i]
+    return near, far, hp
+
+
+def take(mask, n, skip=0):
+    bits = [b for b in range(mask.bit_length()) if (mask >> b) & 1][skip:skip + n]
+    return sum(1 << b for b in bits)
+
+
+def cnt(mask):
+    return bin(mask).count("1")
+
+
+def make_identity(g, T):
+    sm = T.sem
+    g.vector.memset(T.msk[:, :], 0.0).then_inc(sm.z, 1)
+    g.wait_ge(sm.z, 1)
+    g.affine_select(T.msk[:, :], T.msk[:, :], [[-1, 128]], AluOpType.is_equal, -30000.0, 0, 1).then_inc(sm.mk, 1)
+    g.scalar.wait_ge(sm.mk, 1)
+    g.scalar.activation(T.idn[:, :], T.msk[:, :], ActivationFunctionType.Exp).then_inc(sm.id, 1)
+
+
+def serve(g, T, i, qbuf, pre_s, pre_v, dst):
+    sm = T.sem
+    i = str(i)
+    S, O, TP, P, PT, LF = T["s" + i], T["o" + i], T["t" + i], T["p" + i], T["pt" + i], T["lf" + i]
+    for s, n in pre_s:
+        g.tensor.wait_ge(s, n)
+    for h in range(NH):
+        g.tensor.matmul(S[QP * h:QP * h + QP, 0:KP], qbuf[:, QP * h:QP * h + QP], T.ks[:, KP * h:KP * h + KP],
+                        True, True).then_inc(sm["ss" + i], 1)
+    g.vector.wait_ge(sm["ss" + i], NH)
+    g.vector.tensor_reduce(dst[:, COL_M:COL_M + 1], S[:, 0:KP], AxisListType.X, AluOpType.max,
+                           negate=True).then_inc(sm["sm" + i], 1)
+    g.scalar.wait_ge(sm["sm" + i], 1)
+    g.scalar.activation(P[:, :], S[:, 0:KP], ActivationFunctionType.Exp, bias=dst[:, COL_M:COL_M + 1], scale=1.0,
+                        accum_out=LF[:, 0:1]).then_inc(sm["sp" + i], 1)
+    g.tensor.wait_ge(sm["sp" + i], 1)
+    g.tensor.wait_ge(sm.id, 1)
+    g.tensor.transpose(TP[:, 0:128], P[:, :], T.idn[:, :]).then_inc(sm["st" + i], 1)
+    g.vector.wait_ge(sm["sp" + i], 1)
+    g.vector.tensor_copy(dst[:, COL_L:COL_L + 1], LF[:, 0:1]).then_inc(sm["so" + i], 1)
+    g.vector.wait_ge(sm["st" + i], 1)
+    g.vector.tensor_copy(PT[:, :], TP[:, 0:128]).then_inc(sm["sc" + i], 1)
+    g.tensor.wait_ge(sm["sc" + i], 1)
+    for s, n in pre_v:
+        g.tensor.wait_ge(s, n)
+    for h in range(NH):
+        g.tensor.matmul(O[QP * h:QP * h + QP, 0:FD], PT[:, QP * h:QP * h + QP], T.vs[:, FD * h:FD * h + FD],
+                        True, True).then_inc(sm["sv" + i], 1)
+    g.vector.wait_ge(sm["sv" + i], NH)
+    g.vector.tensor_copy(dst[:, 0:FD], O[:, 0:FD]).then_inc(sm["so" + i], 1)
+    return sm["so" + i], 2
+
+
+def xfer(topo, src_core, dst_core, mask, sem, src, dst):
+    rid, pid = topo.addr(dst_core, src_core)
+    return RemoteDMATransfer(dst_ids=[DstId(rid=rid, pnc=pid)], dma_engine_mask=mask, remote_sem=sem, src=src, dst=dst)
+
+
+def helper_program(g, core, T, topo, r, x, peer):
+    sm = T.sem
+    on = topo.mask(r, core)
+    n_q, n_kv = Q_ON, cnt(on) // 2
+    m_peer, m_x = topo.mask(core, peer), topo.mask(core, x)
+    make_identity(g, T)
+    g.wait_ge(sm.aq, n_q)
+    rid, pid = topo.addr(peer, core)
+    g.remote_dma(T.qx[:, :], T.qs[:, :], sm.ax, sm.ls, pid, rid, m_peer)
+    done, n = serve(g, T, 0, T.qx, [(sm.ak, n_kv), (sm.ax, cnt(topo.mask(peer, core)))], [(sm.av, n_kv)], T.snd)
+    g.wait_ge(done, n)
+    rid, pid = topo.addr(x, core)
+    g.remote_dma(T.land[:, T.rank_of(r), 0:WID], T.snd[:, 0:WID], sm.ar, sm.ls, pid, rid, m_x)
+    g.wait_ge(sm.ls, cnt(m_peer) + cnt(m_x))
+
+
+Q_ON = 4
+
+
+def rank_program(g, core, T, topo):
+    near, far, hp = plan(T, topo)
+    for (r, x), d in hp.items():
+        if d == core:
+            helper_program(g, core, T, topo, r, x, hp[(x, r)])
+            return
+    me = T.rank_of(core)
+    if me is None:
+        return
+    sm = T.sem
+    partner = near[core][0]
+    helpers = [hp[(core, x)] for x in far[core]]
+    off = topo.mask(core, partner)
+    on = topo.mask(core, helpers[0])
+    hi = on & ~off
+    halves = [hi, on & off]
+
+    g.sync.dma_start(T.qs[:, :], T.q[:, :]).then_inc(sm.lq, 16)
+    g.scalar.dma_start(T.ks[:, :], T.k[:, :]).then_inc(sm.lk, 16)
+    g.sync.dma_start(T.vs[:, :], T.v[:, :]).then_inc(sm.lv, 16)
+    make_identity(g, T)
+    g.vector.memset(T.one[:, :], 1.0).then_inc(sm.on, 1)
+
+    sent = 0
+    g.wait_ge(sm.lq, 16)
+    tr = [xfer(topo, core, d, take(hi, Q_ON, Q_ON * i), sm.aq, T.qs[:, :], T.qs[:, :]) for i, d in enumerate(helpers)]
+    g.remote_dma_fused(tr, local_sem=sm.ls)
+    sent += Q_ON * len(helpers)
+    rid, pid = topo.addr(partner, core)
+    g.remote_dma(T.qx[:, :], T.qs[:, :], sm.ax, sm.ls, pid, rid, off)
+    sent += cnt(off)
+    for lsem, asem, buf in ((sm.lk, sm.ak, T.ks), (sm.lv, sm.av, T.vs)):
+        g.wait_ge(lsem, 16)
+        tr = [xfer(topo, core, d, halves[i], asem, buf[:, :], buf[:, :]) for i, d in enumerate(helpers)]
+        g.remote_dma_fused(tr, local_sem=sm.ls)
+        sent += sum(cnt(m) for m in halves)
+    g.wait_ge(sm.on, 1)
+    g.affine_select(T.prm[:, :], T.one[:, :], [[-1, QP], [-QP, NH]], AluOpType.is_equal, 0.0, 0, 1).then_inc(sm.pm, 1)
+
+    own_done, own_n = serve(g, T, 0, T.qs, [(sm.lq, 16), (sm.lk, 16)], [(sm.lv, 16)], T.land[:, me, :])
+    done, n = serve(g, T, 1, T.qx, [(sm.ax, cnt(topo.mask(partner, core)))], [], T.snd)
+    g.wait_ge(done, n)
+    g.remote_dma(T.land[:, me, 0:WID], T.snd[:, 0:WID], sm.ar, sm.ls, pid, rid, off)
+    sent += cnt(off)
+
+    n_ar = cnt(topo.mask(partner, core)) + sum(cnt(topo.mask(hp[(x, core)], core)) for x in far[core])
+    g.vector.wait_ge(own_done, own_n)
+    g.vector.wait_ge(sm.ar, n_ar)
+    g.vector.tensor_reduce(T.ngm[:, 0:1], T.land[:, :, COL_M], AxisListType.X, AluOpType.min).then_inc(sm.n, 1)
+    g.scalar.wait_ge(sm.n, 1)
+    g.scalar.wait_ge(sm.ar, n_ar)
+    g.scalar.activation(T.aw[:, 0:4], T.land[:, :, COL_M], ActivationFunctionType.Exp, bias=T.ngm[:, 0:1],
+                        scale=-1.0).then_inc(sm.a, 1)
+    g.vector.wait_ge(sm.a, 1)
+    g.vector.wait_ge(sm.pm, 1)
+    g.tensor.wait_ge(sm.ar, n_ar)
+    g.tensor.wait_ge(own_done, own_n)
+    for j in range(4):
+        g.vector.tensor_scalar(T.dg[:, j, :], T.prm[:, :], T.aw[:, j:j + 1], None, AluOpType.mult).then_inc(sm["d%d" % j], 1)
+        g.tensor.wait_ge(sm["d%d" % j], 1)
+        g.tensor.matmul(T.yp[:, 0:FD + 1], T.dg[:, j, :], T.land[:, j, 0:FD + 1], j == 0, j == 3).then_inc(sm.y, 1)
+    g.vector.wait_ge(sm.y, 4)
+    g.vector.reciprocal(T.rl[:, 0:1], T.yp[:, COL_L:COL_L + 1]).then_inc(sm.r, 1)
+    g.vector.wait_ge(sm.r, 1)
+    g.vector.tensor_scalar(T.ysb[:, :], T.yp[:, 0:FD], T.rl[:, 0:1], None, AluOpType.mult).then_inc(sm.f, 1)
+    g.sync.wait_ge(sm.f, 1)
+    g.sync.dma_start(T.y[:, :], T.ysb[:, :]).then_inc(sm.st, 16)
+    g.sync.wait_ge(sm.st, 16)
+    g.wait_ge(sm.ls, sent)

@@ -2,24 +2,26 @@ from concourse.bass import DstId, RemoteDMATransfer
 from concourse.mybir import AluOpType, AxisListType, ActivationFunctionType
 
 NH, QP, KP, FD = 4, 32, 128, 128
-COL_L, COL_M = FD, FD + 1
-WID = FD + 2
+VO = NH * KP
+WID = FD + 1
 PAD = 136
 
 SCRATCH = {
+    "qd": ("dram", [128, NH * QP], "bfloat16"),
     "qs": ("sbuf", [128, NH * QP], "bfloat16"),
     "qx": ("sbuf", [128, NH * QP], "bfloat16"),
-    "ks": ("sbuf", [128, NH * KP], "bfloat16"),
-    "vs": ("sbuf", [128, NH * FD], "bfloat16"),
-    "msk": ("sbuf", [128, 128], "float32"),
+    "kv": ("sbuf", [128, NH * KP + NH * FD], "bfloat16"),
+    "msk": ("sbuf", [128, 128], "bfloat16"),
     "idn": ("sbuf", [128, 128], "bfloat16"),
-    "one": ("sbuf", [128, 128], "bfloat16"),
+    "one": ("sbuf", [128, 64], "bfloat16"),
     "prm": ("sbuf", [128, 128], "bfloat16"),
     "p0": ("sbuf", [128, KP], "bfloat16"), "p1": ("sbuf", [128, KP], "bfloat16"),
     "pt0": ("sbuf", [128, 128], "bfloat16"), "pt1": ("sbuf", [128, 128], "bfloat16"),
     "lf0": ("sbuf", [128, 4], "float32"), "lf1": ("sbuf", [128, 4], "float32"),
     "land": ("sbuf", [128, 4, PAD], "bfloat16"),
+    "stm": ("sbuf", [128, 4, 8], "bfloat16"),
     "snd": ("sbuf", [128, PAD], "bfloat16"),
+    "ngs": ("sbuf", [128, 8], "bfloat16"),
     "ngm": ("sbuf", [128, 4], "float32"),
     "aw": ("sbuf", [128, 8], "bfloat16"),
     "dg": ("sbuf", [128, 4, 128], "bfloat16"),
@@ -30,8 +32,8 @@ SCRATCH = {
     "t0": ("psum", [128, 1024], "bfloat16"), "t1": ("psum", [128, 1024], "bfloat16"),
     "yp": ("psum", [128, 512], "float32"),
 }
-SEMAPHORES = (["lq", "lk", "lv", "aq", "ak", "av", "ax", "ar", "ls", "z", "mk", "id", "on", "pm",
-               "n", "a", "d0", "d1", "d2", "d3", "y", "r", "f", "st"]
+SEMAPHORES = (["ld", "lq", "lk", "lv", "aq", "ak", "ax", "am", "ms", "ls", "z", "mk", "id", "pm",
+               "n", "a", "d0", "d1", "d2", "d3", "r0", "r1", "r2", "r3", "y", "r", "f", "st"]
               + [s + i for i in "01" for s in ("ss", "sm", "sp", "st", "sc", "sv", "so")])
 
 
@@ -49,55 +51,50 @@ def plan(T, topo):
     return near, far, hp
 
 
-def take(mask, n, skip=0):
-    bits = [b for b in range(mask.bit_length()) if (mask >> b) & 1][skip:skip + n]
-    return sum(1 << b for b in bits)
-
-
 def cnt(mask):
     return bin(mask).count("1")
 
 
-def make_identity(g, T):
-    sm = T.sem
-    g.vector.memset(T.msk[:, :], 0.0).then_inc(sm.z, 1)
-    g.wait_ge(sm.z, 1)
-    g.affine_select(T.msk[:, :], T.msk[:, :], [[-1, 128]], AluOpType.is_equal, -30000.0, 0, 1).then_inc(sm.mk, 1)
-    g.scalar.wait_ge(sm.mk, 1)
-    g.scalar.activation(T.idn[:, :], T.msk[:, :], ActivationFunctionType.Exp).then_inc(sm.id, 1)
-
-
-def serve(g, T, i, qbuf, pre_s, pre_v, dst):
+def serve(g, T, i, qbuf, pre_s, pre_v, dst, md):
     sm = T.sem
     i = str(i)
     S, O, TP, P, PT, LF = T["s" + i], T["o" + i], T["t" + i], T["p" + i], T["pt" + i], T["lf" + i]
     for s, n in pre_s:
         g.tensor.wait_ge(s, n)
     for h in range(NH):
-        g.tensor.matmul(S[QP * h:QP * h + QP, 0:KP], qbuf[:, QP * h:QP * h + QP], T.ks[:, KP * h:KP * h + KP],
+        g.tensor.matmul(S[QP * h:QP * h + QP, 0:KP], qbuf[:, QP * h:QP * h + QP], T.kv[:, KP * h:KP * h + KP],
                         True, True).then_inc(sm["ss" + i], 1)
     g.vector.wait_ge(sm["ss" + i], NH)
-    g.vector.tensor_reduce(dst[:, COL_M:COL_M + 1], S[:, 0:KP], AxisListType.X, AluOpType.max,
-                           negate=True).then_inc(sm["sm" + i], 1)
+    g.vector.tensor_reduce(md, S[:, 0:KP], AxisListType.X, AluOpType.max, negate=True).then_inc(sm["sm" + i], 1)
     g.scalar.wait_ge(sm["sm" + i], 1)
-    g.scalar.activation(P[:, :], S[:, 0:KP], ActivationFunctionType.Exp, bias=dst[:, COL_M:COL_M + 1], scale=1.0,
+    g.scalar.activation(P[:, :], S[:, 0:KP], ActivationFunctionType.Exp, bias=md, scale=1.0,
                         accum_out=LF[:, 0:1]).then_inc(sm["sp" + i], 1)
     g.tensor.wait_ge(sm["sp" + i], 1)
     g.tensor.wait_ge(sm.id, 1)
     g.tensor.transpose(TP[:, 0:128], P[:, :], T.idn[:, :]).then_inc(sm["st" + i], 1)
     g.vector.wait_ge(sm["sp" + i], 1)
-    g.vector.tensor_copy(dst[:, COL_L:COL_L + 1], LF[:, 0:1]).then_inc(sm["so" + i], 1)
+    g.vector.tensor_copy(dst[:, FD:FD + 1], LF[:, 0:1]).then_inc(sm["so" + i], 1)
     g.vector.wait_ge(sm["st" + i], 1)
     g.vector.tensor_copy(PT[:, :], TP[:, 0:128]).then_inc(sm["sc" + i], 1)
     g.tensor.wait_ge(sm["sc" + i], 1)
     for s, n in pre_v:
         g.tensor.wait_ge(s, n)
     for h in range(NH):
-        g.tensor.matmul(O[QP * h:QP * h + QP, 0:FD], PT[:, QP * h:QP * h + QP], T.vs[:, FD * h:FD * h + FD],
+        g.tensor.matmul(O[QP * h:QP * h + QP, 0:FD], PT[:, QP * h:QP * h + QP], T.kv[:, VO + FD * h:VO + FD * h + FD],
                         True, True).then_inc(sm["sv" + i], 1)
     g.vector.wait_ge(sm["sv" + i], NH)
     g.vector.tensor_copy(dst[:, 0:FD], O[:, 0:FD]).then_inc(sm["so" + i], 1)
-    return sm["so" + i], 2
+    return (sm["sm" + i], 1), (sm["so" + i], 2)
+
+
+def send_partial(g, T, topo, core, x, slot, mask, m_done, o_done):
+    sm = T.sem
+    rid, pid = topo.addr(x, core)
+    g.wait_ge(*m_done)
+    g.remote_dma(T.stm[:, slot, 0:1], T.ngs[:, 0:1], sm.am, sm.ls, pid, rid, mask)
+    g.wait_ge(*o_done)
+    g.remote_dma(T.land[:, slot, 0:WID], T.snd[:, 0:WID], sm["r%d" % slot], sm.ls, pid, rid, mask)
+    return 2 * cnt(mask)
 
 
 def xfer(topo, src_core, dst_core, mask, sem, src, dst):
@@ -105,30 +102,33 @@ def xfer(topo, src_core, dst_core, mask, sem, src, dst):
     return RemoteDMATransfer(dst_ids=[DstId(rid=rid, pnc=pid)], dma_engine_mask=mask, remote_sem=sem, src=src, dst=dst)
 
 
-def helper_program(g, core, T, topo, r, x, peer):
+def helper_program(g, core, T, topo, r, x, peer, half):
     sm = T.sem
-    on = topo.mask(r, core)
-    n_q, n_kv = Q_ON, cnt(on) // 2
+    n_on = cnt(topo.mask(r, core)) // 2
     m_peer, m_x = topo.mask(core, peer), topo.mask(core, x)
-    make_identity(g, T)
-    g.wait_ge(sm.aq, n_q)
+    hw = 128 // 2
+    g.vector.memset(T.one[:, 0:hw], 1.0).then_inc(sm.z, 1)
+    g.wait_ge(sm.z, 1)
+    g.affine_select(T.prm[:, 0:hw], T.one[:, 0:hw], [[-1, hw // NH], [-QP, NH]], AluOpType.is_equal, 0.0,
+                    -(hw // NH) * half, 1).then_inc(sm.mk, 1)
+    g.wait_ge(sm.mk, 1)
+    rid, pid = topo.addr(r, core)
+    g.remote_dma(T.prm[:, hw * half:hw * half + hw], T.prm[:, 0:hw], sm.pm, sm.ls, pid, rid, m_peer)
+    g.scalar.wait_ge(sm.ms, n_on)
+    g.scalar.activation(T.idn[:, :], T.msk[:, :], ActivationFunctionType.Exp).then_inc(sm.id, 1)
+    g.wait_ge(sm.aq, n_on)
     rid, pid = topo.addr(peer, core)
-    g.remote_dma(T.qx[:, :], T.qs[:, :], sm.ax, sm.ls, pid, rid, m_peer)
-    done, n = serve(g, T, 0, T.qx, [(sm.ak, n_kv), (sm.ax, cnt(topo.mask(peer, core)))], [(sm.av, n_kv)], T.snd)
-    g.wait_ge(done, n)
-    rid, pid = topo.addr(x, core)
-    g.remote_dma(T.land[:, T.rank_of(r), 0:WID], T.snd[:, 0:WID], sm.ar, sm.ls, pid, rid, m_x)
-    g.wait_ge(sm.ls, cnt(m_peer) + cnt(m_x))
-
-
-Q_ON = 4
+    g.remote_dma(T.qx[:, :], T.qd[:, :], sm.ax, sm.ls, pid, rid, m_peer)
+    m_done, o_done = serve(g, T, 0, T.qx, [(sm.ak, n_on), (sm.ax, cnt(topo.mask(peer, core)))], [], T.snd, T.ngs[:, 0:1])
+    sent = send_partial(g, T, topo, core, x, T.rank_of(r), m_x, m_done, o_done)
+    g.wait_ge(sm.ls, 2 * cnt(m_peer) + sent)
 
 
 def rank_program(g, core, T, topo):
     near, far, hp = plan(T, topo)
     for (r, x), d in hp.items():
         if d == core:
-            helper_program(g, core, T, topo, r, x, hp[(x, r)])
+            helper_program(g, core, T, topo, r, x, hp[(x, r)], far[r].index(x))
             return
     me = T.rank_of(core)
     if me is None:
@@ -138,55 +138,63 @@ def rank_program(g, core, T, topo):
     helpers = [hp[(core, x)] for x in far[core]]
     off = topo.mask(core, partner)
     on = topo.mask(core, helpers[0])
-    hi = on & ~off
-    halves = [hi, on & off]
+    halves = [on & ~off, on & off]
 
-    g.sync.dma_start(T.qs[:, :], T.q[:, :]).then_inc(sm.lq, 16)
-    g.scalar.dma_start(T.ks[:, :], T.k[:, :]).then_inc(sm.lk, 16)
-    g.sync.dma_start(T.vs[:, :], T.v[:, :]).then_inc(sm.lv, 16)
-    make_identity(g, T)
-    g.vector.memset(T.one[:, :], 1.0).then_inc(sm.on, 1)
+    g.sync.dma_start(T.qd[:, :], T.q[:, :]).then_inc(sm.ld, 16)
+    g.scalar.dma_start(T.kv[:, 0:VO], T.k[:, :]).then_inc(sm.lk, 16)
+    g.sync.dma_start(T.kv[:, VO:VO + NH * FD], T.v[:, :]).then_inc(sm.lv, 16)
+    g.scalar.dma_start(T.qs[:, :], T.q[:, :]).then_inc(sm.lq, 16)
+    g.vector.memset(T.msk[:, :], 0.0).then_inc(sm.z, 1)
+    g.wait_ge(sm.z, 1)
+    g.affine_select(T.msk[:, :], T.msk[:, :], [[-1, 128]], AluOpType.is_equal, -30000.0, 0, 1).then_inc(sm.mk, 1)
+    g.wait_ge(sm.mk, 1)
+    g.scalar.wait_ge(sm.mk, 1)
+    g.scalar.activation(T.idn[:, :], T.msk[:, :], ActivationFunctionType.Exp).then_inc(sm.id, 1)
 
-    sent = 0
-    g.wait_ge(sm.lq, 16)
-    tr = [xfer(topo, core, d, take(hi, Q_ON, Q_ON * i), sm.aq, T.qs[:, :], T.qs[:, :]) for i, d in enumerate(helpers)]
-    g.remote_dma_fused(tr, local_sem=sm.ls)
-    sent += Q_ON * len(helpers)
-    rid, pid = topo.addr(partner, core)
-    g.remote_dma(T.qx[:, :], T.qs[:, :], sm.ax, sm.ls, pid, rid, off)
-    sent += cnt(off)
-    for lsem, asem, buf in ((sm.lk, sm.ak, T.ks), (sm.lv, sm.av, T.vs)):
-        g.wait_ge(lsem, 16)
+    def to_helpers(asem, buf):
         tr = [xfer(topo, core, d, halves[i], asem, buf[:, :], buf[:, :]) for i, d in enumerate(helpers)]
         g.remote_dma_fused(tr, local_sem=sm.ls)
-        sent += sum(cnt(m) for m in halves)
-    g.wait_ge(sm.on, 1)
-    g.affine_select(T.prm[:, :], T.one[:, :], [[-1, QP], [-QP, NH]], AluOpType.is_equal, 0.0, 0, 1).then_inc(sm.pm, 1)
+        return sum(cnt(m) for m in halves)
 
-    own_done, own_n = serve(g, T, 0, T.qs, [(sm.lq, 16), (sm.lk, 16)], [(sm.lv, 16)], T.land[:, me, :])
-    done, n = serve(g, T, 1, T.qx, [(sm.ax, cnt(topo.mask(partner, core)))], [], T.snd)
-    g.wait_ge(done, n)
-    g.remote_dma(T.land[:, me, 0:WID], T.snd[:, 0:WID], sm.ar, sm.ls, pid, rid, off)
+    sent = to_helpers(sm.ms, T.msk)
+    g.wait_ge(sm.ld, 16)
+    sent += to_helpers(sm.aq, T.qd)
+    rid, pid = topo.addr(partner, core)
+    g.remote_dma(T.qx[:, :], T.qd[:, :], sm.ax, sm.ls, pid, rid, off)
     sent += cnt(off)
+    g.wait_ge(sm.lk, 16)
+    g.wait_ge(sm.lv, 16)
+    sent += to_helpers(sm.ak, T.kv)
 
-    n_ar = cnt(topo.mask(partner, core)) + sum(cnt(topo.mask(hp[(x, core)], core)) for x in far[core])
-    g.vector.wait_ge(own_done, own_n)
-    g.vector.wait_ge(sm.ar, n_ar)
-    g.vector.tensor_reduce(T.ngm[:, 0:1], T.land[:, :, COL_M], AxisListType.X, AluOpType.min).then_inc(sm.n, 1)
+    own_m, own_o = serve(g, T, 0, T.qs, [(sm.lq, 16), (sm.lk, 16)], [(sm.lv, 16)], T.land[:, me, :], T.stm[:, me, 0:1])
+    m_done, o_done = serve(g, T, 1, T.qx, [(sm.ax, cnt(topo.mask(partner, core)))], [], T.snd, T.ngs[:, 0:1])
+    sent += send_partial(g, T, topo, core, partner, me, off, m_done, o_done)
+
+    src = {T.rank_of(partner): partner}
+    for x in far[core]:
+        src[T.rank_of(x)] = hp[(x, core)]
+    n_am = sum(cnt(topo.mask(d, core)) for d in src.values())
+    n_pm = sum(cnt(topo.mask(d, hp[(x, core)])) for d, x in zip(helpers, far[core]))
+    order = [me] + list(src)
+    g.vector.wait_ge(*own_m)
+    g.vector.wait_ge(sm.am, n_am)
+    g.vector.tensor_reduce(T.ngm[:, 0:1], T.stm[:, :, 0], AxisListType.X, AluOpType.min).then_inc(sm.n, 1)
     g.scalar.wait_ge(sm.n, 1)
-    g.scalar.wait_ge(sm.ar, n_ar)
-    g.scalar.activation(T.aw[:, 0:4], T.land[:, :, COL_M], ActivationFunctionType.Exp, bias=T.ngm[:, 0:1],
+    g.scalar.wait_ge(sm.am, n_am)
+    g.scalar.activation(T.aw[:, 0:4], T.stm[:, :, 0], ActivationFunctionType.Exp, bias=T.ngm[:, 0:1],
                         scale=-1.0).then_inc(sm.a, 1)
     g.vector.wait_ge(sm.a, 1)
-    g.vector.wait_ge(sm.pm, 1)
-    g.tensor.wait_ge(sm.ar, n_ar)
-    g.tensor.wait_ge(own_done, own_n)
-    for j in range(4):
+    g.vector.wait_ge(sm.pm, n_pm)
+    for n, j in enumerate(order):
         g.vector.tensor_scalar(T.dg[:, j, :], T.prm[:, :], T.aw[:, j:j + 1], None, AluOpType.mult).then_inc(sm["d%d" % j], 1)
         g.tensor.wait_ge(sm["d%d" % j], 1)
-        g.tensor.matmul(T.yp[:, 0:FD + 1], T.dg[:, j, :], T.land[:, j, 0:FD + 1], j == 0, j == 3).then_inc(sm.y, 1)
+        if j == me:
+            g.tensor.wait_ge(*own_o)
+        else:
+            g.tensor.wait_ge(sm["r%d" % j], cnt(topo.mask(src[j], core)))
+        g.tensor.matmul(T.yp[:, 0:WID], T.dg[:, j, :], T.land[:, j, 0:WID], n == 0, n == 3).then_inc(sm.y, 1)
     g.vector.wait_ge(sm.y, 4)
-    g.vector.reciprocal(T.rl[:, 0:1], T.yp[:, COL_L:COL_L + 1]).then_inc(sm.r, 1)
+    g.vector.reciprocal(T.rl[:, 0:1], T.yp[:, FD:FD + 1]).then_inc(sm.r, 1)
     g.vector.wait_ge(sm.r, 1)
     g.vector.tensor_scalar(T.ysb[:, :], T.yp[:, 0:FD], T.rl[:, 0:1], None, AluOpType.mult).then_inc(sm.f, 1)
     g.sync.wait_ge(sm.f, 1)

@@ -3,8 +3,8 @@ from concourse.mybir import AluOpType, AxisListType, ActivationFunctionType
 
 NH, QP, KP, FD = 4, 32, 128, 128
 VO = NH * KP
-WID = FD + 1
-PAD = 136
+HF = FD // 2
+B2 = 256
 
 SCRATCH = {
     "qd": ("dram", [128, NH * QP], "bfloat16"),
@@ -18,10 +18,12 @@ SCRATCH = {
     "p0": ("sbuf", [128, KP], "bfloat16"), "p1": ("sbuf", [128, KP], "bfloat16"),
     "pt0": ("sbuf", [128, 128], "bfloat16"), "pt1": ("sbuf", [128, 128], "bfloat16"),
     "lf0": ("sbuf", [128, 4], "float32"), "lf1": ("sbuf", [128, 4], "float32"),
-    "land": ("sbuf", [128, 4, PAD], "bfloat16"),
+    "land": ("sbuf", [128, 4, FD], "bfloat16"),
     "stm": ("sbuf", [128, 4, 8], "bfloat16"),
-    "snd": ("sbuf", [128, PAD], "bfloat16"),
+    "stl": ("sbuf", [128, 4, 8], "bfloat16"),
+    "snd": ("sbuf", [128, FD], "bfloat16"),
     "ngs": ("sbuf", [128, 8], "bfloat16"),
+    "lgs": ("sbuf", [128, 8], "bfloat16"),
     "ngm": ("sbuf", [128, 4], "float32"),
     "aw": ("sbuf", [128, 8], "bfloat16"),
     "dg": ("sbuf", [128, 4, 128], "bfloat16"),
@@ -30,11 +32,11 @@ SCRATCH = {
     "s0": ("psum", [128, 512], "float32"), "s1": ("psum", [128, 512], "float32"),
     "o0": ("psum", [128, 512], "float32"), "o1": ("psum", [128, 512], "float32"),
     "t0": ("psum", [128, 1024], "bfloat16"), "t1": ("psum", [128, 1024], "bfloat16"),
-    "yp": ("psum", [128, 512], "float32"),
+    "yp": ("psum", [128, 512], "float32"), "lp": ("psum", [128, 512], "float32"),
 }
-SEMAPHORES = (["ld", "lq", "lk", "lv", "aq", "ak", "ax", "am", "ms", "ls", "z", "mk", "id", "pm",
-               "n", "a", "d0", "d1", "d2", "d3", "r0", "r1", "r2", "r3", "y", "r", "f", "st"]
-              + [s + i for i in "01" for s in ("ss", "sm", "sp", "st", "sc", "sv", "so")])
+SEMAPHORES = (["ld", "lq", "lk", "lv", "aq", "ak", "ax", "am", "all", "ms", "ls", "z", "mk", "id", "pm",
+               "n", "a", "d0", "d1", "d2", "d3", "r0", "r1", "r2", "r3", "y", "y2", "e1", "r", "f", "st"]
+              + [s + i for i in "01" for s in ("ss", "sm", "sp", "sl", "st", "sc", "sv", "sw", "so")])
 
 
 def plan(T, topo):
@@ -55,7 +57,7 @@ def cnt(mask):
     return bin(mask).count("1")
 
 
-def serve(g, T, i, qbuf, pre_s, pre_v, dst, md):
+def serve(g, T, i, qbuf, pre_s, pre_v, dst, md, ldst, split):
     sm = T.sem
     i = str(i)
     S, O, TP, P, PT, LF = T["s" + i], T["o" + i], T["t" + i], T["p" + i], T["pt" + i], T["lf" + i]
@@ -73,28 +75,40 @@ def serve(g, T, i, qbuf, pre_s, pre_v, dst, md):
     g.tensor.wait_ge(sm.id, 1)
     g.tensor.transpose(TP[:, 0:128], P[:, :], T.idn[:, :]).then_inc(sm["st" + i], 1)
     g.vector.wait_ge(sm["sp" + i], 1)
-    g.vector.tensor_copy(dst[:, FD:FD + 1], LF[:, 0:1]).then_inc(sm["so" + i], 1)
+    g.vector.tensor_copy(ldst, LF[:, 0:1]).then_inc(sm["sl" + i], 1)
     g.vector.wait_ge(sm["st" + i], 1)
     g.vector.tensor_copy(PT[:, :], TP[:, 0:128]).then_inc(sm["sc" + i], 1)
     g.tensor.wait_ge(sm["sc" + i], 1)
     for s, n in pre_v:
         g.tensor.wait_ge(s, n)
-    for h in range(NH):
-        g.tensor.matmul(O[QP * h:QP * h + QP, 0:FD], PT[:, QP * h:QP * h + QP], T.kv[:, VO + FD * h:VO + FD * h + FD],
-                        True, True).then_inc(sm["sv" + i], 1)
+    if not split:
+        for h in range(NH):
+            g.tensor.matmul(O[QP * h:QP * h + QP, 0:FD], PT[:, QP * h:QP * h + QP],
+                            T.kv[:, VO + FD * h:VO + FD * h + FD], True, True).then_inc(sm["sv" + i], 1)
+        g.vector.wait_ge(sm["sv" + i], NH)
+        g.vector.tensor_copy(dst[:, 0:FD], O[:, 0:FD]).then_inc(sm["so" + i], 1)
+        return (sm["sm" + i], 1), (sm["sl" + i], 1), (sm["so" + i], 1)
+    for c, (bank, base, sem) in enumerate(((O, 0, "sv"), (S, B2, "sw"))):
+        for h in range(NH):
+            g.tensor.matmul(bank[QP * h:QP * h + QP, base:base + HF], PT[:, QP * h:QP * h + QP],
+                            T.kv[:, VO + FD * h + HF * c:VO + FD * h + HF * c + HF], True, True).then_inc(sm[sem + i], 1)
     g.vector.wait_ge(sm["sv" + i], NH)
-    g.vector.tensor_copy(dst[:, 0:FD], O[:, 0:FD]).then_inc(sm["so" + i], 1)
-    return (sm["sm" + i], 1), (sm["so" + i], 2)
+    g.vector.tensor_copy(dst[:, 0:HF], O[:, 0:HF]).then_inc(sm["so" + i], 1)
+    g.scalar.wait_ge(sm["sw" + i], NH)
+    g.scalar.activation(dst[:, HF:FD], S[:, B2:B2 + HF], ActivationFunctionType.Copy).then_inc(sm["so" + i], 1)
+    return (sm["sm" + i], 1), (sm["sl" + i], 1), (sm["so" + i], 2)
 
 
-def send_partial(g, T, topo, core, x, slot, mask, m_done, o_done):
+def send_partial(g, T, topo, core, x, slot, mask, m_done, l_done, o_done):
     sm = T.sem
     rid, pid = topo.addr(x, core)
     g.wait_ge(*m_done)
     g.remote_dma(T.stm[:, slot, 0:1], T.ngs[:, 0:1], sm.am, sm.ls, pid, rid, mask)
+    g.wait_ge(*l_done)
+    g.remote_dma(T.stl[:, slot, 0:1], T.lgs[:, 0:1], sm.all, sm.ls, pid, rid, mask)
     g.wait_ge(*o_done)
-    g.remote_dma(T.land[:, slot, 0:WID], T.snd[:, 0:WID], sm["r%d" % slot], sm.ls, pid, rid, mask)
-    return 2 * cnt(mask)
+    g.remote_dma(T.land[:, slot, :], T.snd[:, :], sm["r%d" % slot], sm.ls, pid, rid, mask)
+    return 3 * cnt(mask)
 
 
 def xfer(topo, src_core, dst_core, mask, sem, src, dst):
@@ -119,8 +133,9 @@ def helper_program(g, core, T, topo, r, x, peer, half):
     g.wait_ge(sm.aq, n_on)
     rid, pid = topo.addr(peer, core)
     g.remote_dma(T.qx[:, :], T.qd[:, :], sm.ax, sm.ls, pid, rid, m_peer)
-    m_done, o_done = serve(g, T, 0, T.qx, [(sm.ak, n_on), (sm.ax, cnt(topo.mask(peer, core)))], [], T.snd, T.ngs[:, 0:1])
-    sent = send_partial(g, T, topo, core, x, T.rank_of(r), m_x, m_done, o_done)
+    done = serve(g, T, 0, T.qx, [(sm.ak, n_on), (sm.ax, cnt(topo.mask(peer, core)))], [], T.snd,
+                 T.ngs[:, 0:1], T.lgs[:, 0:1], True)
+    sent = send_partial(g, T, topo, core, x, T.rank_of(r), m_x, *done)
     g.wait_ge(sm.ls, 2 * cnt(m_peer) + sent)
 
 
@@ -166,9 +181,10 @@ def rank_program(g, core, T, topo):
     g.wait_ge(sm.lv, 16)
     sent += to_helpers(sm.ak, T.kv)
 
-    own_m, own_o = serve(g, T, 0, T.qs, [(sm.lq, 16), (sm.lk, 16)], [(sm.lv, 16)], T.land[:, me, :], T.stm[:, me, 0:1])
-    m_done, o_done = serve(g, T, 1, T.qx, [(sm.ax, cnt(topo.mask(partner, core)))], [], T.snd, T.ngs[:, 0:1])
-    sent += send_partial(g, T, topo, core, partner, me, off, m_done, o_done)
+    own_m, own_l, own_o = serve(g, T, 0, T.qs, [(sm.lq, 16), (sm.lk, 16)], [(sm.lv, 16)], T.land[:, me, :],
+                                T.stm[:, me, 0:1], T.stl[:, me, 0:1], False)
+    done = serve(g, T, 1, T.qx, [(sm.ax, cnt(topo.mask(partner, core)))], [], T.snd, T.ngs[:, 0:1], T.lgs[:, 0:1], False)
+    sent += send_partial(g, T, topo, core, partner, me, off, *done)
 
     src = {T.rank_of(partner): partner}
     for x in far[core]:
@@ -185,19 +201,38 @@ def rank_program(g, core, T, topo):
                         scale=-1.0).then_inc(sm.a, 1)
     g.vector.wait_ge(sm.a, 1)
     g.vector.wait_ge(sm.pm, n_pm)
-    for n, j in enumerate(order):
+    Y2 = T.o0
+    for j in order:
         g.vector.tensor_scalar(T.dg[:, j, :], T.prm[:, :], T.aw[:, j:j + 1], None, AluOpType.mult).then_inc(sm["d%d" % j], 1)
+
+    def add_o(n, j):
         g.tensor.wait_ge(sm["d%d" % j], 1)
         if j == me:
             g.tensor.wait_ge(*own_o)
         else:
             g.tensor.wait_ge(sm["r%d" % j], cnt(topo.mask(src[j], core)))
-        g.tensor.matmul(T.yp[:, 0:WID], T.dg[:, j, :], T.land[:, j, 0:WID], n == 0, n == 3).then_inc(sm.y, 1)
-    g.vector.wait_ge(sm.y, 4)
-    g.vector.reciprocal(T.rl[:, 0:1], T.yp[:, FD:FD + 1]).then_inc(sm.r, 1)
+        g.tensor.matmul(T.yp[:, 0:HF], T.dg[:, j, :], T.land[:, j, 0:HF], n == 0, n == 3).then_inc(sm.y, 1)
+        g.tensor.matmul(Y2[:, B2:B2 + HF], T.dg[:, j, :], T.land[:, j, HF:FD], n == 0, n == 3).then_inc(sm.y2, 1)
+
+    add_o(0, order[0])
+    add_o(1, order[1])
+    g.tensor.wait_ge(*own_l)
+    g.tensor.wait_ge(sm.all, n_am)
+    for n, j in enumerate(order):
+        g.tensor.wait_ge(sm["d%d" % j], 1)
+        g.tensor.matmul(T.lp[:, 0:1], T.dg[:, j, :], T.stl[:, j, 0:1], n == 0, n == 3).then_inc(sm.e1, 1)
+    add_o(2, order[2])
+    add_o(3, order[3])
+    g.vector.wait_ge(sm.e1, 4)
+    g.vector.reciprocal(T.rl[:, 0:1], T.lp[:, 0:1]).then_inc(sm.r, 1)
     g.vector.wait_ge(sm.r, 1)
-    g.vector.tensor_scalar(T.ysb[:, :], T.yp[:, 0:FD], T.rl[:, 0:1], None, AluOpType.mult).then_inc(sm.f, 1)
-    g.sync.wait_ge(sm.f, 1)
+    g.vector.wait_ge(sm.y, 4)
+    g.vector.tensor_scalar(T.ysb[:, 0:HF], T.yp[:, 0:HF], T.rl[:, 0:1], None, AluOpType.mult).then_inc(sm.f, 1)
+    g.scalar.wait_ge(sm.r, 1)
+    g.scalar.wait_ge(sm.y2, 4)
+    g.scalar.activation(T.ysb[:, HF:FD], Y2[:, B2:B2 + HF], ActivationFunctionType.Copy,
+                        scale=T.rl[:, 0:1]).then_inc(sm.f, 1)
+    g.sync.wait_ge(sm.f, 2)
     g.sync.dma_start(T.y[:, :], T.ysb[:, :]).then_inc(sm.st, 16)
     g.sync.wait_ge(sm.st, 16)
     g.wait_ge(sm.ls, sent)

@@ -11,6 +11,9 @@ SCRATCH = {
     "qs": ("sbuf", [128, NH * QP], "bfloat16"),
     "qx": ("sbuf", [128, NH * QP], "bfloat16"),
     "kv": ("sbuf", [128, NH * KP + NH * FD], "bfloat16"),
+    "pc": ("sbuf", [128, 8], "bfloat16"),
+    "on2": ("sbuf", [128, 128], "bfloat16"),
+    "rw": ("sbuf", [128, 128], "bfloat16"),
     "msk": ("sbuf", [128, 128], "bfloat16"),
     "idn": ("sbuf", [128, 128], "bfloat16"),
     "one": ("sbuf", [128, 64], "bfloat16"),
@@ -34,8 +37,8 @@ SCRATCH = {
     "t0": ("psum", [128, 1024], "bfloat16"), "t1": ("psum", [128, 1024], "bfloat16"),
     "yp": ("psum", [128, 512], "float32"), "lp": ("psum", [128, 512], "float32"),
 }
-SEMAPHORES = (["ld", "lq", "lk", "lv", "aq", "ak", "ax", "am", "all", "ms", "ls", "z", "mk", "id", "pm",
-               "n", "a", "d0", "d1", "d2", "d3", "r0", "r1", "r2", "r3", "y", "y2", "e1", "r", "f", "st"]
+SEMAPHORES = (["ld", "lq", "lk", "lv", "aq", "ak", "av", "ax", "am", "all", "ms", "ls", "z", "z1", "z2", "mk", "mk2", "id",
+               "pm", "n", "a", "d0", "d1", "d2", "d3", "r0", "r1", "r2", "r3", "y", "y2", "e1", "r", "f", "st"]
               + [s + i for i in "01" for s in ("ss", "sm", "sp", "sl", "st", "sc", "sv", "sw", "so")])
 
 
@@ -55,6 +58,19 @@ def plan(T, topo):
 
 def cnt(mask):
     return bin(mask).count("1")
+
+
+def identity(g, T, pc_sem, pc_n):
+    sm = T.sem
+    g.vector.memset(T.on2[:, :], 1.0).then_inc(sm.z1, 1)
+    g.vector.wait_ge(sm.z1, 1)
+    g.vector.tensor_tensor_scan(T.rw[:, :], T.on2[:, :], T.on2[:, :], 0.0, AluOpType.mult, AluOpType.add).then_inc(sm.z2, 1)
+    g.vector.wait_ge(sm.z2, 1)
+    g.vector.wait_ge(pc_sem, pc_n)
+    g.vector.tensor_scalar(T.msk[:, :], T.rw[:, :], T.pc[:, 0:1], -30000.0, AluOpType.not_equal,
+                           AluOpType.mult).then_inc(sm.mk2, 1)
+    g.scalar.wait_ge(sm.mk2, 1)
+    g.scalar.activation(T.idn[:, :], T.msk[:, :], ActivationFunctionType.Exp).then_inc(sm.id, 1)
 
 
 def serve(g, T, i, qbuf, pre_s, pre_v, dst, md, ldst, split):
@@ -128,12 +144,11 @@ def helper_program(g, core, T, topo, r, x, peer, half):
     g.wait_ge(sm.mk, 1)
     rid, pid = topo.addr(r, core)
     g.remote_dma(T.prm[:, hw * half:hw * half + hw], T.prm[:, 0:hw], sm.pm, sm.ls, pid, rid, m_peer)
-    g.scalar.wait_ge(sm.ms, n_on)
-    g.scalar.activation(T.idn[:, :], T.msk[:, :], ActivationFunctionType.Exp).then_inc(sm.id, 1)
+    identity(g, T, sm.ms, n_on)
     g.wait_ge(sm.aq, n_on)
     rid, pid = topo.addr(peer, core)
     g.remote_dma(T.qx[:, :], T.qd[:, :], sm.ax, sm.ls, pid, rid, m_peer)
-    done = serve(g, T, 0, T.qx, [(sm.ak, n_on), (sm.ax, cnt(topo.mask(peer, core)))], [], T.snd,
+    done = serve(g, T, 0, T.qx, [(sm.ak, n_on), (sm.ax, cnt(topo.mask(peer, core)))], [(sm.av, n_on)], T.snd,
                  T.ngs[:, 0:1], T.lgs[:, 0:1], True)
     sent = send_partial(g, T, topo, core, x, T.rank_of(r), m_x, *done)
     g.wait_ge(sm.ls, 2 * cnt(m_peer) + sent)
@@ -159,27 +174,25 @@ def rank_program(g, core, T, topo):
     g.scalar.dma_start(T.kv[:, 0:VO], T.k[:, :]).then_inc(sm.lk, 16)
     g.sync.dma_start(T.kv[:, VO:VO + NH * FD], T.v[:, :]).then_inc(sm.lv, 16)
     g.scalar.dma_start(T.qs[:, :], T.q[:, :]).then_inc(sm.lq, 16)
-    g.vector.memset(T.msk[:, :], 0.0).then_inc(sm.z, 1)
-    g.wait_ge(sm.z, 1)
-    g.affine_select(T.msk[:, :], T.msk[:, :], [[-1, 128]], AluOpType.is_equal, -30000.0, 0, 1).then_inc(sm.mk, 1)
+    g.iota(T.pc[:, 0:1], [[1, 1]], 1, 1, allow_small_or_imprecise_dtypes=True).then_inc(sm.mk, 1)
     g.wait_ge(sm.mk, 1)
-    g.scalar.wait_ge(sm.mk, 1)
-    g.scalar.activation(T.idn[:, :], T.msk[:, :], ActivationFunctionType.Exp).then_inc(sm.id, 1)
 
     def to_helpers(asem, buf):
-        tr = [xfer(topo, core, d, halves[i], asem, buf[:, :], buf[:, :]) for i, d in enumerate(helpers)]
+        tr = [xfer(topo, core, d, halves[i], asem, buf, buf) for i, d in enumerate(helpers)]
         g.remote_dma_fused(tr, local_sem=sm.ls)
         return sum(cnt(m) for m in halves)
 
-    sent = to_helpers(sm.ms, T.msk)
+    sent = to_helpers(sm.ms, T.pc[:, 0:1])
+    identity(g, T, sm.mk, 1)
     g.wait_ge(sm.ld, 16)
-    sent += to_helpers(sm.aq, T.qd)
+    sent += to_helpers(sm.aq, T.qd[:, :])
     rid, pid = topo.addr(partner, core)
     g.remote_dma(T.qx[:, :], T.qd[:, :], sm.ax, sm.ls, pid, rid, off)
     sent += cnt(off)
     g.wait_ge(sm.lk, 16)
+    sent += to_helpers(sm.ak, T.kv[:, 0:VO])
     g.wait_ge(sm.lv, 16)
-    sent += to_helpers(sm.ak, T.kv)
+    sent += to_helpers(sm.av, T.kv[:, VO:VO + NH * FD])
 
     own_m, own_l, own_o = serve(g, T, 0, T.qs, [(sm.lq, 16), (sm.lk, 16)], [(sm.lv, 16)], T.land[:, me, :],
                                 T.stm[:, me, 0:1], T.stl[:, me, 0:1], False)

from concourse.bass import DstId, RemoteDMATransfer
from concourse.mybir import AluOpType, AxisListType, ActivationFunctionType

NH, QP, KP, FD = 4, 32, 128, 128
VO = NH * KP
HF = FD // 2
B2 = 256

SCRATCH = {
    "qd": ("dram", [128, NH * QP], "bfloat16"),
    "qs": ("sbuf", [128, NH * QP], "bfloat16"),
    "qx": ("sbuf", [128, NH * QP], "bfloat16"),
    "kv": ("sbuf", [128, NH * KP + NH * FD], "bfloat16"),
    "pc": ("sbuf", [128, 8], "bfloat16"),
    "on2": ("sbuf", [128, 128], "bfloat16"),
    "rw": ("sbuf", [128, 128], "bfloat16"),
    "msk": ("sbuf", [128, 128], "bfloat16"),
    "idn": ("sbuf", [128, 128], "bfloat16"),
    "one": ("sbuf", [128, 64], "bfloat16"),
    "prm": ("sbuf", [128, 128], "bfloat16"),
    "p0": ("sbuf", [128, KP], "bfloat16"), "p1": ("sbuf", [128, KP], "bfloat16"),
    "pt0": ("sbuf", [128, 128], "bfloat16"), "pt1": ("sbuf", [128, 128], "bfloat16"),
    "lf0": ("sbuf", [128, 4], "float32"), "lf1": ("sbuf", [128, 4], "float32"),
    "land": ("sbuf", [128, 4, FD], "bfloat16"),
    "stm": ("sbuf", [128, 4, 8], "bfloat16"),
    "stl": ("sbuf", [128, 4, 8], "bfloat16"),
    "snd": ("sbuf", [128, FD], "bfloat16"),
    "ngs": ("sbuf", [128, 8], "bfloat16"),
    "lgs": ("sbuf", [128, 8], "bfloat16"),
    "ngm": ("sbuf", [128, 4], "float32"),
    "aw": ("sbuf", [128, 8], "bfloat16"),
    "dg": ("sbuf", [128, 4, 128], "bfloat16"),
    "rl": ("sbuf", [128, 4], "float32"),
    "ysb": ("sbuf", [128, FD], "bfloat16"),
    "s0": ("psum", [128, 512], "float32"), "s1": ("psum", [128, 512], "float32"),
    "o0": ("psum", [128, 512], "float32"), "o1": ("psum", [128, 512], "float32"),
    "t0": ("psum", [128, 1024], "bfloat16"), "t1": ("psum", [128, 1024], "bfloat16"),
    "yp": ("psum", [128, 512], "float32"), "lp": ("psum", [128, 512], "float32"),
}
SEMAPHORES = (["ld", "lq", "lk", "lv", "aq", "ak", "av", "ax", "am", "all", "ms", "ls", "z", "z1", "z2", "mk", "mk2", "id",
               "pm", "n", "a", "d0", "d1", "d2", "d3", "r0", "r1", "r2", "r3", "y", "y2", "e1", "r", "f", "st"]
              + [s + i for i in "01" for s in ("ss", "sm", "sp", "sl", "st", "sc", "sv", "sw", "so")])


def plan(T, topo):
    cores = list(T.cores)
    world = range((max(topo.host(c) for c in cores) + 1) * topo.CORES_PER_HOST)
    near, far, hp = {}, {}, {}
    for r in cores:
        near[r] = [x for x in cores if x != r and topo.may_write(r, x)]
        far[r] = [x for x in cores if x != r and not topo.may_write(r, x)]
        own = [d for d in world if d not in cores and topo.host(d) == topo.host(r) and topo.chip(d) == topo.chip(r)
               and topo.die(d) == topo.die(r) and all(topo.may_write(d, x) for x in far[r])]
        for i, x in enumerate(far[r]):
            hp[(r, x)] = own[i]
    return near, far, hp


def cnt(mask):
    return bin(mask).count("1")


def identity(g, T, pc_sem, pc_n):
    sm = T.sem
    g.vector.memset(T.on2[:, :], 1.0).then_inc(sm.z1, 1)
    g.vector.wait_ge(sm.z1, 1)
    g.vector.tensor_tensor_scan(T.rw[:, :], T.on2[:, :], T.on2[:, :], 0.0, AluOpType.mult, AluOpType.add).then_inc(sm.z2, 1)
    g.vector.wait_ge(sm.z2, 1)
    g.vector.wait_ge(pc_sem, pc_n)
    g.vector.tensor_scalar(T.msk[:, :], T.rw[:, :], T.pc[:, 0:1], -30000.0, AluOpType.not_equal,
                           AluOpType.mult).then_inc(sm.mk2, 1)
    g.scalar.wait_ge(sm.mk2, 1)
    g.scalar.activation(T.idn[:, :], T.msk[:, :], ActivationFunctionType.Exp).then_inc(sm.id, 1)


def serve(g, T, i, qbuf, pre_s, pre_v, dst, md, ldst, split):
    sm = T.sem
    i = str(i)
    S, O, TP, P, PT, LF = T["s" + i], T["o" + i], T["t" + i], T["p" + i], T["pt" + i], T["lf" + i]
    for s, n in pre_s:
        g.tensor.wait_ge(s, n)
    for h in range(NH):
        g.tensor.matmul(S[QP * h:QP * h + QP, 0:KP], qbuf[:, QP * h:QP * h + QP], T.kv[:, KP * h:KP * h + KP],
                        True, True).then_inc(sm["ss" + i], 1)
    g.vector.wait_ge(sm["ss" + i], NH)
    g.vector.tensor_reduce(md, S[:, 0:KP], AxisListType.X, AluOpType.max, negate=True).then_inc(sm["sm" + i], 1)
    g.scalar.wait_ge(sm["sm" + i], 1)
    g.scalar.activation(P[:, :], S[:, 0:KP], ActivationFunctionType.Exp, bias=md, scale=1.0,
                        accum_out=LF[:, 0:1]).then_inc(sm["sp" + i], 1)
    g.tensor.wait_ge(sm["sp" + i], 1)
    g.tensor.wait_ge(sm.id, 1)
    g.tensor.transpose(TP[:, 0:128], P[:, :], T.idn[:, :]).then_inc(sm["st" + i], 1)
    g.vector.wait_ge(sm["sp" + i], 1)
    g.vector.tensor_copy(ldst, LF[:, 0:1]).then_inc(sm["sl" + i], 1)
    g.vector.wait_ge(sm["st" + i], 1)
    g.vector.tensor_copy(PT[:, :], TP[:, 0:128]).then_inc(sm["sc" + i], 1)
    g.tensor.wait_ge(sm["sc" + i], 1)
    for s, n in pre_v:
        g.tensor.wait_ge(s, n)
    if not split:
        for h in range(NH):
            g.tensor.matmul(O[QP * h:QP * h + QP, 0:FD], PT[:, QP * h:QP * h + QP],
                            T.kv[:, VO + FD * h:VO + FD * h + FD], True, True).then_inc(sm["sv" + i], 1)
        g.vector.wait_ge(sm["sv" + i], NH)
        g.vector.tensor_copy(dst[:, 0:FD], O[:, 0:FD]).then_inc(sm["so" + i], 1)
        return (sm["sm" + i], 1), (sm["sl" + i], 1), (sm["so" + i], 1)
    for c, (bank, base, sem) in enumerate(((O, 0, "sv"), (S, B2, "sw"))):
        for h in range(NH):
            g.tensor.matmul(bank[QP * h:QP * h + QP, base:base + HF], PT[:, QP * h:QP * h + QP],
                            T.kv[:, VO + FD * h + HF * c:VO + FD * h + HF * c + HF], True, True).then_inc(sm[sem + i], 1)
    g.vector.wait_ge(sm["sv" + i], NH)
    g.vector.tensor_copy(dst[:, 0:HF], O[:, 0:HF]).then_inc(sm["so" + i], 1)
    g.scalar.wait_ge(sm["sw" + i], NH)
    g.scalar.activation(dst[:, HF:FD], S[:, B2:B2 + HF], ActivationFunctionType.Copy).then_inc(sm["so" + i], 1)
    return (sm["sm" + i], 1), (sm["sl" + i], 1), (sm["so" + i], 2)


def send_partial(g, T, topo, core, x, slot, mask, m_done, l_done, o_done):
    sm = T.sem
    rid, pid = topo.addr(x, core)
    g.wait_ge(*m_done)
    g.remote_dma(T.stm[:, slot, 0:1], T.ngs[:, 0:1], sm.am, sm.ls, pid, rid, mask)
    g.wait_ge(*l_done)
    g.remote_dma(T.stl[:, slot, 0:1], T.lgs[:, 0:1], sm.all, sm.ls, pid, rid, mask)
    g.wait_ge(*o_done)
    g.remote_dma(T.land[:, slot, :], T.snd[:, :], sm["r%d" % slot], sm.ls, pid, rid, mask)
    return 3 * cnt(mask)


def xfer(topo, src_core, dst_core, mask, sem, src, dst):
    rid, pid = topo.addr(dst_core, src_core)
    return RemoteDMATransfer(dst_ids=[DstId(rid=rid, pnc=pid)], dma_engine_mask=mask, remote_sem=sem, src=src, dst=dst)


def helper_program(g, core, T, topo, r, x, peer, half):
    sm = T.sem
    n_on = cnt(topo.mask(r, core)) // 2
    m_peer, m_x = topo.mask(core, peer), topo.mask(core, x)
    hw = 128 // 2
    g.vector.memset(T.one[:, 0:hw], 1.0).then_inc(sm.z, 1)
    g.wait_ge(sm.z, 1)
    g.affine_select(T.prm[:, 0:hw], T.one[:, 0:hw], [[-1, hw // NH], [-QP, NH]], AluOpType.is_equal, 0.0,
                    -(hw // NH) * half, 1).then_inc(sm.mk, 1)
    g.wait_ge(sm.mk, 1)
    rid, pid = topo.addr(r, core)
    g.remote_dma(T.prm[:, hw * half:hw * half + hw], T.prm[:, 0:hw], sm.pm, sm.ls, pid, rid, m_peer)
    identity(g, T, sm.ms, n_on)
    g.wait_ge(sm.aq, n_on)
    rid, pid = topo.addr(peer, core)
    g.remote_dma(T.qx[:, :], T.qd[:, :], sm.ax, sm.ls, pid, rid, m_peer)
    done = serve(g, T, 0, T.qx, [(sm.ak, n_on), (sm.ax, cnt(topo.mask(peer, core)))], [(sm.av, n_on)], T.snd,
                 T.ngs[:, 0:1], T.lgs[:, 0:1], True)
    sent = send_partial(g, T, topo, core, x, T.rank_of(r), m_x, *done)
    g.wait_ge(sm.ls, 2 * cnt(m_peer) + sent)


def rank_program(g, core, T, topo):
    near, far, hp = plan(T, topo)
    for (r, x), d in hp.items():
        if d == core:
            helper_program(g, core, T, topo, r, x, hp[(x, r)], far[r].index(x))
            return
    me = T.rank_of(core)
    if me is None:
        return
    sm = T.sem
    partner = near[core][0]
    helpers = [hp[(core, x)] for x in far[core]]
    off = topo.mask(core, partner)
    on = topo.mask(core, helpers[0])
    halves = [on & ~off, on & off]

    g.sync.dma_start(T.qd[:, :], T.q[:, :]).then_inc(sm.ld, 16)
    g.scalar.dma_start(T.kv[:, 0:VO], T.k[:, :]).then_inc(sm.lk, 16)
    g.sync.dma_start(T.kv[:, VO:VO + NH * FD], T.v[:, :]).then_inc(sm.lv, 16)
    g.scalar.dma_start(T.qs[:, :], T.q[:, :]).then_inc(sm.lq, 16)
    g.iota(T.pc[:, 0:1], [[1, 1]], 1, 1, allow_small_or_imprecise_dtypes=True).then_inc(sm.mk, 1)
    g.wait_ge(sm.mk, 1)

    def to_helpers(asem, buf):
        tr = [xfer(topo, core, d, halves[i], asem, buf, buf) for i, d in enumerate(helpers)]
        g.remote_dma_fused(tr, local_sem=sm.ls)
        return sum(cnt(m) for m in halves)

    sent = to_helpers(sm.ms, T.pc[:, 0:1])
    identity(g, T, sm.mk, 1)
    g.wait_ge(sm.ld, 16)
    sent += to_helpers(sm.aq, T.qd[:, :])
    rid, pid = topo.addr(partner, core)
    g.remote_dma(T.qx[:, :], T.qd[:, :], sm.ax, sm.ls, pid, rid, off)
    sent += cnt(off)
    g.wait_ge(sm.lk, 16)
    sent += to_helpers(sm.ak, T.kv[:, 0:VO])
    g.wait_ge(sm.lv, 16)
    sent += to_helpers(sm.av, T.kv[:, VO:VO + NH * FD])

    own_m, own_l, own_o = serve(g, T, 0, T.qs, [(sm.lq, 16), (sm.lk, 16)], [(sm.lv, 16)], T.land[:, me, :],
                                T.stm[:, me, 0:1], T.stl[:, me, 0:1], False)
    done = serve(g, T, 1, T.qx, [(sm.ax, cnt(topo.mask(partner, core)))], [], T.snd, T.ngs[:, 0:1], T.lgs[:, 0:1], False)
    sent += send_partial(g, T, topo, core, partner, me, off, *done)

    src = {T.rank_of(partner): partner}
    for x in far[core]:
        src[T.rank_of(x)] = hp[(x, core)]
    n_am = sum(cnt(topo.mask(d, core)) for d in src.values())
    n_pm = sum(cnt(topo.mask(d, hp[(x, core)])) for d, x in zip(helpers, far[core]))
    order = [me] + list(src)
    g.vector.wait_ge(*own_m)
    g.vector.wait_ge(sm.am, n_am)
    g.vector.tensor_reduce(T.ngm[:, 0:1], T.stm[:, :, 0], AxisListType.X, AluOpType.min).then_inc(sm.n, 1)
    g.scalar.wait_ge(sm.n, 1)
    g.scalar.wait_ge(sm.am, n_am)
    g.scalar.activation(T.aw[:, 0:4], T.stm[:, :, 0], ActivationFunctionType.Exp, bias=T.ngm[:, 0:1],
                        scale=-1.0).then_inc(sm.a, 1)
    g.vector.wait_ge(sm.a, 1)
    g.vector.wait_ge(sm.pm, n_pm)
    Y2 = T.o0
    for j in order:
        g.vector.tensor_scalar(T.dg[:, j, :], T.prm[:, :], T.aw[:, j:j + 1], None, AluOpType.mult).then_inc(sm["d%d" % j], 1)

    def add_o(n, j):
        g.tensor.wait_ge(sm["d%d" % j], 1)
        if j == me:
            g.tensor.wait_ge(*own_o)
        else:
            g.tensor.wait_ge(sm["r%d" % j], cnt(topo.mask(src[j], core)))
        g.tensor.matmul(T.yp[:, 0:HF], T.dg[:, j, :], T.land[:, j, 0:HF], n == 0, n == 3).then_inc(sm.y, 1)
        g.tensor.matmul(Y2[:, B2:B2 + HF], T.dg[:, j, :], T.land[:, j, HF:FD], n == 0, n == 3).then_inc(sm.y2, 1)

    add_o(0, order[0])
    add_o(1, order[1])
    g.tensor.wait_ge(*own_l)
    g.tensor.wait_ge(sm.all, n_am)
    for n, j in enumerate(order):
        g.tensor.wait_ge(sm["d%d" % j], 1)
        g.tensor.matmul(T.lp[:, 0:1], T.dg[:, j, :], T.stl[:, j, 0:1], n == 0, n == 3).then_inc(sm.e1, 1)
    add_o(2, order[2])
    add_o(3, order[3])
    g.vector.wait_ge(sm.e1, 4)
    g.vector.reciprocal(T.rl[:, 0:1], T.lp[:, 0:1]).then_inc(sm.r, 1)
    g.vector.wait_ge(sm.r, 1)
    g.vector.wait_ge(sm.y, 4)
    g.vector.tensor_scalar(T.ysb[:, 0:HF], T.yp[:, 0:HF], T.rl[:, 0:1], None, AluOpType.mult).then_inc(sm.f, 1)
    g.scalar.wait_ge(sm.r, 1)
    g.scalar.wait_ge(sm.y2, 4)
    g.scalar.activation(T.ysb[:, HF:FD], Y2[:, B2:B2 + HF], ActivationFunctionType.Copy,
                        scale=T.rl[:, 0:1]).then_inc(sm.f, 1)
    g.sync.wait_ge(sm.f, 2)
    g.sync.dma_start(T.y[:, :], T.ysb[:, :]).then_inc(sm.st, 16)
    g.sync.wait_ge(sm.st, 16)
    g.wait_ge(sm.ls, sent)
